import numpy as np
import ml_dtypes


def mxq(x, axis, fmt="e4m3"):
    dtype, down = {"e4m3": (ml_dtypes.float8_e4m3fn, 7), "e5m2": (ml_dtypes.float8_e5m2, 14)}[fmt]
    v = np.moveaxis(np.asarray(x, np.float32).astype(ml_dtypes.bfloat16).astype(np.float64), axis, -1)
    blocks = v.reshape(v.shape[:-1] + (-1, 32))
    amax = np.abs(blocks).max(-1, keepdims=True)
    byte = np.maximum(np.where(amax > 0, np.frexp(amax)[1] - 1 + 127, 0) - down, 1)
    scale = np.exp2(byte - 127.0)
    codes = (blocks / scale).astype(np.float32).astype(dtype).astype(np.float64)
    return np.moveaxis((codes * scale).reshape(v.shape), -1, axis)


WIDE = False


def mx_kscale(k):
    if not WIDE:
        return np.ones(k)
    levels = np.array([10, -10, 5, -5, 0])
    if k % 512:
        return np.exp2(np.random.permutation(np.resize(levels, k // 32))).repeat(32)
    a = np.empty((k // 512, 16))
    for p in range(k // 512):
        a[p, :8] = np.random.permutation(np.resize(levels, 8))
        for g in range(8):
            far = levels[np.abs(levels - a[p, g]) >= 10]
            a[p, g + 8] = far[np.random.randint(len(far))]
    return np.exp2(a.ravel()).repeat(32)


def f64(x):
    return np.asarray(x).astype(np.float64)


def striped(idx):
    return np.tile(idx.reshape(-1, 16).T, (8, 1)).astype(np.uint16)


def unstriped(offs):
    return offs[:16].T.reshape(-1).astype(np.int64)


E2M1 = np.array([0.0, 0.5, 1.0, 1.5, 2.0, 3.0, 4.0, 6.0, -0.0, -0.5, -1.0, -1.5, -2.0, -3.0, -4.0, -6.0])


def pack_weight(w, fmt):
    k, n = w.shape
    w = f64(np.asarray(w, np.float32).astype(ml_dtypes.bfloat16)).reshape(k // 32, 32, n)
    amax = np.abs(w).max(1)
    if fmt == "e4m3":
        byte = np.frexp(amax)[1] - 1 + 127 - 7
    else:
        mant, ex = np.frexp(amax / 6.0)
        byte = np.where(mant > 0.5, ex, ex - 1) + 127
    byte = np.clip(np.where(amax > 0, byte, 1), 1, 254)
    scaled = (w * np.exp2(127.0 - byte)[:, None, :]).reshape(k, n).astype(np.float32)
    by_word = np.ascontiguousarray(scaled.reshape(k // 512, 128, 4, n).transpose(0, 1, 3, 2))
    if fmt == "e4m3":
        words = by_word.astype(ml_dtypes.float8_e4m3fn).view(np.uint8)
    else:
        c = by_word.astype(ml_dtypes.float4_e2m1fn).view(np.uint8) & 0xF
        words = (c[..., 0::2] | (c[..., 1::2] << 4)).reshape(k // 512, 128, 2 * n)
    return np.ascontiguousarray(words), np.ascontiguousarray(byte.astype(np.uint8).reshape(k // 512, 16, n))


def unpack_weight(words, scales, fmt):
    g, _, n = scales.shape
    words = np.ascontiguousarray(words).reshape(g, 128, n, -1)
    if fmt == "e4m3":
        vals = words.view(ml_dtypes.float8_e4m3fn).astype(np.float64)
    else:
        nib = np.empty((g, 128, n, 4), np.uint8)
        nib[..., 0::2] = words & 0xF
        nib[..., 1::2] = words >> 4
        vals = E2M1[nib]
    vals = vals * np.repeat(np.exp2(scales.astype(np.float64) - 127.0), 8, axis=1)[..., None]
    return vals.transpose(0, 1, 3, 2).reshape(g * 512, n)


def gelu(v):
    return 0.5 * v * (1.0 + np.tanh(np.sqrt(2.0 / np.pi) * (v + 0.044715 * v**3)))


K, K1, K2, T, S, S2 = 1024, 512, 512, 2048, 1024, 512


def setup_inputs():
    n = np.random.standard_normal
    s = mx_kscale(K)[:, None]
    d = {}
    d["tab_words"], d["tab_scales"] = pack_weight(n((K, T)) * s, "e4m3")
    d["offs"] = striped(np.random.permutation(T)[:S])
    d["offs2"] = striped(np.random.permutation(T)[:S2])
    d["w1"] = (1.4 * n((K1, K)) / K**0.5 / s[:K1]).astype(np.float32)
    d["w4_words"], d["w4_scales"] = pack_weight(1.4 * n((K2, K)) / K**0.5 / s[K1:], "e2m1")
    d["gain"] = (1.5 * np.exp(0.4 * n(K)) / K**0.5 / s[:, 0]).astype(np.float32)
    d["prox"] = np.exp(0.5 - 2.0 * np.random.uniform(0.0, 1.0, (S2, S))).astype(np.float32)
    d["base"] = (0.6 * n(S2)).astype(np.float32)
    return d


def reference(tab_words, tab_scales, offs, offs2, w1, w4_words, w4_scales, gain, prox, base):
    tw = unpack_weight(tab_words, tab_scales, "e4m3")
    v = tw[:, unstriped(offs)]
    v2 = tw[:, unstriped(offs2)]
    w1q = mxq(f64(w1), 0, "e4m3")
    w4 = unpack_weight(w4_words, w4_scales, "e2m1")
    a = w1q.T @ v[:K1] + w4.T @ v[K1:]
    h = np.tanh(a) * f64(gain)[:, None]
    hq = mxq(h, 0, "e4m3")
    e = v2.T @ hq
    return e * f64(prox) + f64(base)[:, None]

@@ -1,0 +1,206 @@
+from contextlib import ExitStack
+
+import concourse.mybir as mybir
+
+K, T, S, S2 = 1024, 2048, 1024, 512
+FLOPS = 2 * K * K * S + 2 * K * S2 * S
+
+F32 = mybir.dt.float32
+BF16 = mybir.dt.bfloat16
+I32 = mybir.dt.int32
+U32 = mybir.dt.uint32
+U16 = mybir.dt.uint16
+U8 = mybir.dt.uint8
+FP8X4 = mybir.dt.float8_e4m3fn_x4
+FP4X4 = mybir.dt.float4_e2m1fn_x4
+ACT = mybir.ActivationFunctionType
+ALU = mybir.AluOpType
+
+P = 128
+PACK = 4
+KP = P * PACK
+HALF = S // 2
+CH = 256
+UN = 128
+ROW0 = (4, 0)
+
+
+def tile_list_neighbour_crop_scores_kernel(tc, tab_words, tab_scales, offs, offs2, w1, w4_words, w4_scales, gain, prox, base, out):
+    nc = tc.nc
+    with ExitStack() as ctx:
+        keep = ctx.enter_context(tc.tile_pool(name="keep", bufs=1))
+        stage = ctx.enter_context(tc.tile_pool(name="stage", bufs=2))
+        ring = ctx.enter_context(tc.tile_pool(name="ring", bufs=3))
+        psum = ctx.enter_context(tc.psum_pool(name="psum", bufs=4))
+
+        idx = keep.tile([P, S // 16], U16, name="idx")
+        idx2 = keep.tile([P, S2 // 16], U16, name="idx2")
+        tw = [keep.tile([P, T], I32, name="tw%d" % a, align_bytes=64) for a in range(2)]
+        ts = keep.tile([P, T], U8, name="ts", align_bytes=64)
+        w4raw = keep.tile([P, 2 * K], U8, name="w4raw", align_bytes=64)
+        w4sraw = keep.tile([P, K], U8, name="w4sraw", align_bytes=64)
+        zero = keep.tile([P, 1], F32, name="zero", tag="small")
+        zero_bias = keep.tile([P, 1], F32, name="zero_bias")
+
+        nc.vector.memset(ts[:].bitcast(I32), 0)
+        nc.gpsimd.memset(w4sraw[:].bitcast(I32), 0)
+        nc.vector.memset(zero[:], 0.0)
+
+        def load_words(a):
+            nc.sync.dma_start(tw[a][:], tab_words[a].rearrange("p t i -> p (t i)").bitcast(I32))
+
+        def load_w1(b):
+            raw = stage.tile([P, PACK, KP], F32, name="big")
+            nc.sync.dma_start(raw[:], w1.rearrange("(p j) c -> p j c", j=PACK)[:, :, KP * b : KP * (b + 1)])
+            return raw
+
+        nc.sync.dma_start(idx[:], offs)
+        load_words(1)
+        for q in range(4):
+            r = 32 * q + ROW0[1]
+            nc.scalar.dma_start(ts[r : r + 4, :].bitcast(I32), tab_scales[1, 4 * q : 4 * q + 4, :].bitcast(I32))
+        for q in range(4):
+            r = 32 * q + ROW0[0]
+            nc.gpsimd.dma_start(ts[r : r + 4, :].bitcast(I32), tab_scales[0, 4 * q : 4 * q + 4, :].bitcast(I32))
+        nc.sync.dma_start(idx2[:], offs2)
+        w1raw = [load_w1(0)]
+        load_words(0)
+        nc.sync.dma_start(w4raw[:].bitcast(I32), w4_words[0].bitcast(I32))
+        w1raw.append(load_w1(1))
+        for q in range(4):
+            nc.gpsimd.dma_start(w4sraw[32 * q : 32 * q + 4, :].bitcast(I32), w4_scales[0, 4 * q : 4 * q + 4, :].bitcast(I32))
+        nc.scalar.activation(zero_bias[:], zero[:], ACT.Tanh)
+        consts = keep.tile([P, 4, PACK], F32, name="consts", tag="small")
+        gain_t = consts[:, 0:2, :]
+        base_t = consts[:, 2, :]
+        nc.sync.dma_start(gain_t, gain.rearrange("(b p t) -> p b t", b=2, t=PACK))
+        with nc.allow_non_contiguous_dma(reason="one offset for each output row"):
+            nc.sync.dma_start(base_t, base.rearrange("(u p) -> p u", p=P))
+
+        def gather(name, window, dtype, offsets):
+            n = 16 * offsets.shape[1]
+            g = keep.tile([P, n], dtype, name=name, align_bytes=64)
+            nc.vector.tensor_copy(g[:], window.indirect(offsets))
+            return g
+
+        cols = HALF // 16
+        wins = [tw[a][:].bitcast(U32) for a in range(2)]
+        vw = {}
+        vs = {}
+        v2w = {}
+        vw[1, 0] = gather("vw10", wins[1], U32, idx[:, 0:cols])
+        vw[1, 1] = gather("vw11", wins[1], U32, idx[:, cols : 2 * cols])
+        v2w[1] = gather("v2w1", wins[1], U32, idx2[:])
+        vs[0] = gather("vs0", ts[:], U8, idx[:, 0:cols])
+        vw[0, 0] = gather("vw00", wins[0], U32, idx[:, 0:cols])
+
+        w4c = keep.tile([P, 2 * K], U8, name="w4c", align_bytes=64)
+        w4s = keep.tile([P, K], U8, name="w4s", align_bytes=64)
+        nc.vector.tensor_copy(
+            w4c[:].bitcast(U16).rearrange("p (b t m) -> p b t m", b=2, t=PACK),
+            w4raw[:].bitcast(U16).rearrange("p (b m t) -> p b t m", b=2, t=PACK),
+        )
+        nc.vector.tensor_copy(
+            w4s[:].rearrange("p (b t m) -> p b t m", b=2, t=PACK),
+            w4sraw[:].rearrange("p (b m t) -> p b t m", b=2, t=PACK),
+        )
+
+        w1c = {}
+        w1s = {}
+
+        def quantise_w1(b):
+            wb = stage.tile([P, KP * PACK], BF16, name="wb", align_bytes=64)
+            nc.scalar.copy(
+                wb[:].rearrange("p (t m j) -> p m j t", t=PACK, j=PACK),
+                w1raw[b][:].rearrange("p j (m t) -> p m j t", t=PACK),
+            )
+            w1c[b] = keep.tile([P, KP], U32, name="w1c%d" % b, align_bytes=64)
+            w1s[b] = keep.tile([P, KP], U8, name="w1s%d" % b, align_bytes=64)
+            nc.vector.quantize_mx(w1c[b][:].bitcast(FP8X4), w1s[b][:], wb[:])
+
+        prox_t = {}
+
+        def load_prox(h):
+            prox_t[h] = stage.tile([P, PACK, HALF], F32, name="big")
+            nc.sync.dma_start(prox_t[h][:], prox.rearrange("(u p) j -> p u j", p=P)[:, :, HALF * h : HALF * (h + 1)])
+
+        hc = {}
+        hs = {}
+
+        def features(b, c):
+            th = ring.tile([P, CH, PACK], F32, name="th")
+            h, j0 = divmod(CH * c, HALF)
+            for i in range(CH // UN):
+                js = slice(j0 + UN * i, j0 + UN * (i + 1))
+                acc = psum.tile([P, PACK, UN], F32, name="acc")
+                for t in range(PACK):
+                    m0 = P * t
+                    nc.tensor.matmul_mx(
+                        acc[:, t, :],
+                        lhsT=w1c[b][:, m0 : m0 + P].bitcast(FP8X4),
+                        lhsT_scale=w1s[b][:, m0 : m0 + P],
+                        rhs=vw[0, h][:, js].bitcast(FP8X4),
+                        rhs_scale=vs[h][ROW0[0] : P, js],
+                        start=True,
+                        stop=False,
+                    )
+                    r0 = KP * b + m0
+                    nc.tensor.matmul_mx(
+                        acc[:, t, :],
+                        lhsT=w4c[:, 2 * r0 : 2 * (r0 + P)].bitcast(FP4X4),
+                        lhsT_scale=w4s[:, r0 : r0 + P],
+                        rhs=vw[1, h][:, js].bitcast(FP8X4),
+                        rhs_scale=vs[h][ROW0[1] : P, js],
+                        start=False,
+                        stop=True,
+                    )
+                nc.scalar.activation(th[:, UN * i : UN * (i + 1), :], acc[:].rearrange("p t n -> p n t"), ACT.Tanh, bias=zero_bias[:])
+            hb = ring.tile([P, CH, PACK], BF16, name="hb", align_bytes=64)
+            nc.vector.tensor_tensor(hb[:], th[:], gain_t[:, b, :].unsqueeze(1).to_broadcast([P, CH, PACK]), ALU.mult)
+            hc[b, c] = keep.tile([P, CH], U32, name="hc%d%d" % (b, c), align_bytes=64)
+            hs[b, c] = keep.tile([P, CH], U8, name="hs%d%d" % (b, c), align_bytes=64)
+            nc.vector.quantize_mx(hc[b, c][:].bitcast(FP8X4), hs[b, c][:], hb[:].rearrange("p n t -> p (n t)"))
+
+        def scores(c):
+            h, j0 = divmod(CH * c, HALF)
+            res = ring.tile([P, PACK, CH], F32, name="res")
+            for u0 in range(0, PACK, 2):
+                e = psum.tile([P, 2, CH], F32, name="e")
+                for u in range(u0, u0 + 2):
+                    ms = slice(P * u, P * (u + 1))
+                    for a in range(2):
+                        nc.tensor.matmul_mx(
+                            e[:, u - u0, :],
+                            lhsT=v2w[a][:, ms].bitcast(FP8X4),
+                            lhsT_scale=v2s[ROW0[a] : P, ms],
+                            rhs=hc[a, c][:].bitcast(FP8X4),
+                            rhs_scale=hs[a, c][:],
+                            start=(a == 0),
+                            stop=(a == 1),
+                        )
+                pe = ring.tile([P, 2, CH], F32, name="pe")
+                nc.vector.tensor_tensor(pe[:], e[:], prox_t[h][:, u0 : u0 + 2, j0 : j0 + CH], ALU.mult)
+                for u in range(u0, u0 + 2):
+                    nc.scalar.activation(res[:, u, :], pe[:, u - u0, :], ACT.Identity, bias=base_t[:, u : u + 1])
+            nc.sync.dma_start(out.rearrange("(u p) j -> p u j", p=P)[:, :, CH * c : CH * (c + 1)], res[:])
+
+        quantise_w1(0)
+        load_prox(0)
+        vs[1] = gather("vs1", ts[:], U8, idx[:, cols : 2 * cols])
+        features(0, 0)
+        quantise_w1(1)
+        load_prox(1)
+        v2s = gather("v2s", ts[:], U8, idx2[:])
+        features(0, 1)
+        v2w[0] = gather("v2w0", wins[0], U32, idx2[:])
+        features(1, 0)
+        vw[0, 1] = gather("vw01", wins[0], U32, idx[:, cols : 2 * cols])
+        features(1, 1)
+        scores(0)
+        features(0, 2)
+        scores(1)
+        features(1, 2)
+        features(0, 3)
+        scores(2)
+        features(1, 3)
+        scores(3)

@@ -20,7 +20,7 @@ P = 128
 PACK = 4
 KP = P * PACK
 HALF = S // 2
-CH = 256
+CHUNKS = (256, 256, 256, 128, 128)
 UN = 128
 ROW0 = (4, 0)
 
@@ -30,7 +30,7 @@ def tile_list_neighbour_crop_scores_kernel(tc, tab_words, tab_scales, offs, offs
     with ExitStack() as ctx:
         keep = ctx.enter_context(tc.tile_pool(name="keep", bufs=1))
         stage = ctx.enter_context(tc.tile_pool(name="stage", bufs=2))
-        ring = ctx.enter_context(tc.tile_pool(name="ring", bufs=3))
+        ring = ctx.enter_context(tc.tile_pool(name="ring", bufs=4))
         psum = ctx.enter_context(tc.psum_pool(name="psum", bufs=4))
 
         idx = keep.tile([P, S // 16], U16, name="idx")
@@ -39,12 +39,14 @@ def tile_list_neighbour_crop_scores_kernel(tc, tab_words, tab_scales, offs, offs
         ts = keep.tile([P, T], U8, name="ts", align_bytes=64)
         w4raw = keep.tile([P, 2 * K], U8, name="w4raw", align_bytes=64)
         w4sraw = keep.tile([P, K], U8, name="w4sraw", align_bytes=64)
-        zero = keep.tile([P, 1], F32, name="zero", tag="small")
+        gain_t = keep.tile([P, 2, PACK], F32, name="gain_t")
+        base_t = keep.tile([P, PACK], F32, name="base_t")
+        zero = keep.tile([P, 1], F32, name="zero")
         zero_bias = keep.tile([P, 1], F32, name="zero_bias")
 
         nc.vector.memset(ts[:].bitcast(I32), 0)
-        nc.gpsimd.memset(w4sraw[:].bitcast(I32), 0)
         nc.vector.memset(zero[:], 0.0)
+        nc.vector.memset(w4sraw[:].bitcast(I32), 0)
 
         def load_words(a):
             nc.sync.dma_start(tw[a][:], tab_words[a].rearrange("p t i -> p (t i)").bitcast(I32))
@@ -54,28 +56,28 @@ def tile_list_neighbour_crop_scores_kernel(tc, tab_words, tab_scales, offs, offs
             nc.sync.dma_start(raw[:], w1.rearrange("(p j) c -> p j c", j=PACK)[:, :, KP * b : KP * (b + 1)])
             return raw
 
+        def load_scales(n):
+            a, q = divmod(n, 4)
+            r = 32 * q + ROW0[a]
+            nc.sync.dma_start(ts[r : r + 4, :].bitcast(I32), tab_scales[a, 4 * q : 4 * q + 4, :].bitcast(I32))
+
         nc.sync.dma_start(idx[:], offs)
         load_words(1)
-        for q in range(4):
-            r = 32 * q + ROW0[1]
-            nc.scalar.dma_start(ts[r : r + 4, :].bitcast(I32), tab_scales[1, 4 * q : 4 * q + 4, :].bitcast(I32))
-        for q in range(4):
-            r = 32 * q + ROW0[0]
-            nc.gpsimd.dma_start(ts[r : r + 4, :].bitcast(I32), tab_scales[0, 4 * q : 4 * q + 4, :].bitcast(I32))
-        nc.sync.dma_start(idx2[:], offs2)
+        for n in range(5):
+            load_scales(n)
         w1raw = [load_w1(0)]
+        for n in range(5, 8):
+            load_scales(n)
         load_words(0)
-        nc.sync.dma_start(w4raw[:].bitcast(I32), w4_words[0].bitcast(I32))
-        w1raw.append(load_w1(1))
         for q in range(4):
-            nc.gpsimd.dma_start(w4sraw[32 * q : 32 * q + 4, :].bitcast(I32), w4_scales[0, 4 * q : 4 * q + 4, :].bitcast(I32))
-        nc.scalar.activation(zero_bias[:], zero[:], ACT.Tanh)
-        consts = keep.tile([P, 4, PACK], F32, name="consts", tag="small")
-        gain_t = consts[:, 0:2, :]
-        base_t = consts[:, 2, :]
-        nc.sync.dma_start(gain_t, gain.rearrange("(b p t) -> p b t", b=2, t=PACK))
+            nc.sync.dma_start(w4sraw[32 * q : 32 * q + 4, :].bitcast(I32), w4_scales[0, 4 * q : 4 * q + 4, :].bitcast(I32))
+        w1raw.append(load_w1(1))
+        nc.sync.dma_start(w4raw[:].bitcast(I32), w4_words[0].bitcast(I32))
+        nc.sync.dma_start(idx2[:], offs2)
+        nc.sync.dma_start(gain_t[:], gain.rearrange("(b p t) -> p b t", b=2, t=PACK))
         with nc.allow_non_contiguous_dma(reason="one offset for each output row"):
-            nc.sync.dma_start(base_t, base.rearrange("(u p) -> p u", p=P))
+            nc.sync.dma_start(base_t[:], base.rearrange("(u p) -> p u", p=P))
+        nc.scalar.activation(zero_bias[:], zero[:], ACT.Tanh)
 
         def gather(name, window, dtype, offsets):
             n = 16 * offsets.shape[1]
@@ -83,27 +85,11 @@ def tile_list_neighbour_crop_scores_kernel(tc, tab_words, tab_scales, offs, offs
             nc.vector.tensor_copy(g[:], window.indirect(offsets))
             return g
 
-        cols = HALF // 16
         wins = [tw[a][:].bitcast(U32) for a in range(2)]
         vw = {}
-        vs = {}
         v2w = {}
-        vw[1, 0] = gather("vw10", wins[1], U32, idx[:, 0:cols])
-        vw[1, 1] = gather("vw11", wins[1], U32, idx[:, cols : 2 * cols])
-        v2w[1] = gather("v2w1", wins[1], U32, idx2[:])
-        vs[0] = gather("vs0", ts[:], U8, idx[:, 0:cols])
-        vw[0, 0] = gather("vw00", wins[0], U32, idx[:, 0:cols])
-
-        w4c = keep.tile([P, 2 * K], U8, name="w4c", align_bytes=64)
-        w4s = keep.tile([P, K], U8, name="w4s", align_bytes=64)
-        nc.vector.tensor_copy(
-            w4c[:].bitcast(U16).rearrange("p (b t m) -> p b t m", b=2, t=PACK),
-            w4raw[:].bitcast(U16).rearrange("p (b m t) -> p b t m", b=2, t=PACK),
-        )
-        nc.vector.tensor_copy(
-            w4s[:].rearrange("p (b t m) -> p b t m", b=2, t=PACK),
-            w4sraw[:].rearrange("p (b m t) -> p b t m", b=2, t=PACK),
-        )
+        vw[1] = gather("vw1", wins[1], U32, idx[:])
+        vs = gather("vs", ts[:], U8, idx[:])
 
         w1c = {}
         w1s = {}
@@ -118,19 +104,35 @@ def tile_list_neighbour_crop_scores_kernel(tc, tab_words, tab_scales, offs, offs
             w1s[b] = keep.tile([P, KP], U8, name="w1s%d" % b, align_bytes=64)
             nc.vector.quantize_mx(w1c[b][:].bitcast(FP8X4), w1s[b][:], wb[:])
 
+        quantise_w1(0)
+        vw[0] = gather("vw0", wins[0], U32, idx[:])
+
+        w4c = keep.tile([P, 2 * K], U8, name="w4c", align_bytes=64)
+        w4s = keep.tile([P, K], U8, name="w4s", align_bytes=64)
+        nc.vector.tensor_copy(
+            w4c[:].bitcast(U16).rearrange("p (b t m) -> p b t m", b=2, t=PACK),
+            w4raw[:].bitcast(U16).rearrange("p (b m t) -> p b t m", b=2, t=PACK),
+        )
+        nc.vector.tensor_copy(
+            w4s[:].rearrange("p (b t m) -> p b t m", b=2, t=PACK),
+            w4sraw[:].rearrange("p (b m t) -> p b t m", b=2, t=PACK),
+        )
+
         prox_t = {}
 
         def load_prox(h):
             prox_t[h] = stage.tile([P, PACK, HALF], F32, name="big")
             nc.sync.dma_start(prox_t[h][:], prox.rearrange("(u p) j -> p u j", p=P)[:, :, HALF * h : HALF * (h + 1)])
 
+        hb = {}
         hc = {}
         hs = {}
 
         def features(b, c):
-            th = ring.tile([P, CH, PACK], F32, name="th")
-            h, j0 = divmod(CH * c, HALF)
-            for i in range(CH // UN):
+            n = CHUNKS[c]
+            th = ring.tile([P, n, PACK], F32, name="th")
+            j0 = sum(CHUNKS[:c])
+            for i in range(n // UN):
                 js = slice(j0 + UN * i, j0 + UN * (i + 1))
                 acc = psum.tile([P, PACK, UN], F32, name="acc")
                 for t in range(PACK):
@@ -139,8 +141,8 @@ def tile_list_neighbour_crop_scores_kernel(tc, tab_words, tab_scales, offs, offs
                         acc[:, t, :],
                         lhsT=w1c[b][:, m0 : m0 + P].bitcast(FP8X4),
                         lhsT_scale=w1s[b][:, m0 : m0 + P],
-                        rhs=vw[0, h][:, js].bitcast(FP8X4),
-                        rhs_scale=vs[h][ROW0[0] : P, js],
+                        rhs=vw[0][:, js].bitcast(FP8X4),
+                        rhs_scale=vs[ROW0[0] : P, js],
                         start=True,
                         stop=False,
                     )
@@ -149,23 +151,27 @@ def tile_list_neighbour_crop_scores_kernel(tc, tab_words, tab_scales, offs, offs
                         acc[:, t, :],
                         lhsT=w4c[:, 2 * r0 : 2 * (r0 + P)].bitcast(FP4X4),
                         lhsT_scale=w4s[:, r0 : r0 + P],
-                        rhs=vw[1, h][:, js].bitcast(FP8X4),
-                        rhs_scale=vs[h][ROW0[1] : P, js],
+                        rhs=vw[1][:, js].bitcast(FP8X4),
+                        rhs_scale=vs[ROW0[1] : P, js],
                         start=False,
                         stop=True,
                     )
                 nc.scalar.activation(th[:, UN * i : UN * (i + 1), :], acc[:].rearrange("p t n -> p n t"), ACT.Tanh, bias=zero_bias[:])
-            hb = ring.tile([P, CH, PACK], BF16, name="hb", align_bytes=64)
-            nc.vector.tensor_tensor(hb[:], th[:], gain_t[:, b, :].unsqueeze(1).to_broadcast([P, CH, PACK]), ALU.mult)
-            hc[b, c] = keep.tile([P, CH], U32, name="hc%d%d" % (b, c), align_bytes=64)
-            hs[b, c] = keep.tile([P, CH], U8, name="hs%d%d" % (b, c), align_bytes=64)
-            nc.vector.quantize_mx(hc[b, c][:].bitcast(FP8X4), hs[b, c][:], hb[:].rearrange("p n t -> p (n t)"))
+            hb[b, c] = ring.tile([P, n, PACK], BF16, name="hb", align_bytes=64)
+            nc.vector.tensor_tensor(hb[b, c][:], th[:], gain_t[:, b, :].unsqueeze(1).to_broadcast([P, n, PACK]), ALU.mult)
+
+        def quantise_h(b, c):
+            n = CHUNKS[c]
+            hc[b, c] = keep.tile([P, n], U32, name="hc%d%d" % (b, c), align_bytes=64)
+            hs[b, c] = keep.tile([P, n], U8, name="hs%d%d" % (b, c), align_bytes=64)
+            nc.vector.quantize_mx(hc[b, c][:].bitcast(FP8X4), hs[b, c][:], hb[b, c][:].rearrange("p n t -> p (n t)"))
 
         def scores(c):
-            h, j0 = divmod(CH * c, HALF)
-            res = ring.tile([P, PACK, CH], F32, name="res")
+            n = CHUNKS[c]
+            start = sum(CHUNKS[:c])
+            h, j0 = divmod(start, HALF)
             for u0 in range(0, PACK, 2):
-                e = psum.tile([P, 2, CH], F32, name="e")
+                e = psum.tile([P, 2, n], F32, name="e")
                 for u in range(u0, u0 + 2):
                     ms = slice(P * u, P * (u + 1))
                     for a in range(2):
@@ -178,29 +184,28 @@ def tile_list_neighbour_crop_scores_kernel(tc, tab_words, tab_scales, offs, offs
                             start=(a == 0),
                             stop=(a == 1),
                         )
-                pe = ring.tile([P, 2, CH], F32, name="pe")
-                nc.vector.tensor_tensor(pe[:], e[:], prox_t[h][:, u0 : u0 + 2, j0 : j0 + CH], ALU.mult)
+                pe = ring.tile([P, 2, n], F32, name="pe")
+                res = ring.tile([P, 2, n], F32, name="res")
+                nc.vector.tensor_tensor(pe[:], e[:], prox_t[h][:, u0 : u0 + 2, j0 : j0 + n], ALU.mult)
                 for u in range(u0, u0 + 2):
-                    nc.scalar.activation(res[:, u, :], pe[:, u - u0, :], ACT.Identity, bias=base_t[:, u : u + 1])
-            nc.sync.dma_start(out.rearrange("(u p) j -> p u j", p=P)[:, :, CH * c : CH * (c + 1)], res[:])
+                    nc.scalar.activation(res[:, u - u0, :], pe[:, u - u0, :], ACT.Identity, bias=base_t[:, u : u + 1])
+                nc.sync.dma_start(out.rearrange("(u p) j -> p u j", p=P)[:, u0 : u0 + 2, start : start + n], res[:])
 
-        quantise_w1(0)
-        load_prox(0)
-        vs[1] = gather("vs1", ts[:], U8, idx[:, cols : 2 * cols])
-        features(0, 0)
         quantise_w1(1)
-        load_prox(1)
         v2s = gather("v2s", ts[:], U8, idx2[:])
-        features(0, 1)
+        v2w[1] = gather("v2w1", wins[1], U32, idx2[:])
         v2w[0] = gather("v2w0", wins[0], U32, idx2[:])
-        features(1, 0)
-        vw[0, 1] = gather("vw01", wins[0], U32, idx[:, cols : 2 * cols])
-        features(1, 1)
-        scores(0)
-        features(0, 2)
-        scores(1)
-        features(1, 2)
-        features(0, 3)
-        scores(2)
-        features(1, 3)
-        scores(3)
+        load_prox(0)
+        load_prox(1)
+        last = len(CHUNKS) - 1
+        for c in range(len(CHUNKS)):
+            features(0, c)
+            if c > 0:
+                quantise_h(1, c - 1)
+            features(1, c)
+            quantise_h(0, c)
+            if 0 < c < last:
+                scores(c - 1)
+        quantise_h(1, last)
+        scores(last - 1)
+        scores(last)

@@ -61,18 +61,22 @@ def tile_list_neighbour_crop_scores_kernel(tc, tab_words, tab_scales, offs, offs
             r = 32 * q + ROW0[a]
             nc.sync.dma_start(ts[r : r + 4, :].bitcast(I32), tab_scales[a, 4 * q : 4 * q + 4, :].bitcast(I32))
 
+        def load_w4_scales(q):
+            nc.sync.dma_start(w4sraw[32 * q : 32 * q + 4, :].bitcast(I32), w4_scales[0, 4 * q : 4 * q + 4, :].bitcast(I32))
+
         nc.sync.dma_start(idx[:], offs)
         load_words(1)
         for n in range(5):
             load_scales(n)
-        w1raw = [load_w1(0)]
+        load_words(0)
         for n in range(5, 8):
             load_scales(n)
-        load_words(0)
-        for q in range(4):
-            nc.sync.dma_start(w4sraw[32 * q : 32 * q + 4, :].bitcast(I32), w4_scales[0, 4 * q : 4 * q + 4, :].bitcast(I32))
-        w1raw.append(load_w1(1))
+        w1raw = [load_w1(0)]
         nc.sync.dma_start(w4raw[:].bitcast(I32), w4_words[0].bitcast(I32))
+        for q in range(3):
+            load_w4_scales(q)
+        w1raw.append(load_w1(1))
+        load_w4_scales(3)
         nc.sync.dma_start(idx2[:], offs2)
         nc.sync.dma_start(gain_t[:], gain.rearrange("(b p t) -> p b t", b=2, t=PACK))
         with nc.allow_non_contiguous_dma(reason="one offset for each output row"):
@@ -89,6 +93,7 @@ def tile_list_neighbour_crop_scores_kernel(tc, tab_words, tab_scales, offs, offs
         vw = {}
         v2w = {}
         vw[1] = gather("vw1", wins[1], U32, idx[:])
+        vw[0] = gather("vw0", wins[0], U32, idx[:])
         vs = gather("vs", ts[:], U8, idx[:])
 
         w1c = {}
@@ -97,15 +102,13 @@ def tile_list_neighbour_crop_scores_kernel(tc, tab_words, tab_scales, offs, offs
         def quantise_w1(b):
             wb = stage.tile([P, KP * PACK], BF16, name="wb", align_bytes=64)
             nc.scalar.copy(
-                wb[:].rearrange("p (t m j) -> p m j t", t=PACK, j=PACK),
-                w1raw[b][:].rearrange("p j (m t) -> p m j t", t=PACK),
+                wb[:].rearrange("p (th tl m j) -> p th m j tl", th=2, tl=2, j=PACK),
+                w1raw[b][:].rearrange("p j (m th tl) -> p th m j tl", th=2, tl=2),
             )
             w1c[b] = keep.tile([P, KP], U32, name="w1c%d" % b, align_bytes=64)
             w1s[b] = keep.tile([P, KP], U8, name="w1s%d" % b, align_bytes=64)
             nc.vector.quantize_mx(w1c[b][:].bitcast(FP8X4), w1s[b][:], wb[:])
 
-        quantise_w1(0)
-        vw[0] = gather("vw0", wins[0], U32, idx[:])
 
         w4c = keep.tile([P, 2 * K], U8, name="w4c", align_bytes=64)
         w4s = keep.tile([P, K], U8, name="w4s", align_bytes=64)
@@ -113,6 +116,7 @@ def tile_list_neighbour_crop_scores_kernel(tc, tab_words, tab_scales, offs, offs
             w4c[:].bitcast(U16).rearrange("p (b t m) -> p b t m", b=2, t=PACK),
             w4raw[:].bitcast(U16).rearrange("p (b m t) -> p b t m", b=2, t=PACK),
         )
+        quantise_w1(0)
         nc.vector.tensor_copy(
             w4s[:].rearrange("p (b t m) -> p b t m", b=2, t=PACK),
             w4sraw[:].rearrange("p (b m t) -> p b t m", b=2, t=PACK),
@@ -188,7 +192,10 @@ def tile_list_neighbour_crop_scores_kernel(tc, tab_words, tab_scales, offs, offs
                 res = ring.tile([P, 2, n], F32, name="res")
                 nc.vector.tensor_tensor(pe[:], e[:], prox_t[h][:, u0 : u0 + 2, j0 : j0 + n], ALU.mult)
                 for u in range(u0, u0 + 2):
-                    nc.scalar.activation(res[:, u - u0, :], pe[:, u - u0, :], ACT.Identity, bias=base_t[:, u : u + 1])
+                    if c == len(CHUNKS) - 1 and u == PACK - 1:
+                        nc.vector.tensor_scalar(res[:, u - u0, :], pe[:, u - u0, :], base_t[:, u : u + 1], None, ALU.add)
+                    else:
+                        nc.scalar.activation(res[:, u - u0, :], pe[:, u - u0, :], ACT.Identity, bias=base_t[:, u : u + 1])
                 nc.sync.dma_start(out.rearrange("(u p) j -> p u j", p=P)[:, u0 : u0 + 2, start : start + n], res[:])
 
         quantise_w1(1)

@@ -20,8 +20,6 @@ P = 128
 PACK = 4
 KP = P * PACK
 HALF = S // 2
-CHUNKS = (256, 256, 256, 128, 128)
-UN = 128
 ROW0 = (4, 0)
 
 
@@ -30,8 +28,7 @@ def tile_list_neighbour_crop_scores_kernel(tc, tab_words, tab_scales, offs, offs
     with ExitStack() as ctx:
         keep = ctx.enter_context(tc.tile_pool(name="keep", bufs=1))
         stage = ctx.enter_context(tc.tile_pool(name="stage", bufs=2))
-        ring = ctx.enter_context(tc.tile_pool(name="ring", bufs=4))
-        psum = ctx.enter_context(tc.psum_pool(name="psum", bufs=4))
+        psum = ctx.enter_context(tc.psum_pool(name="psum", bufs=8))
 
         idx = keep.tile([P, S // 16], U16, name="idx")
         idx2 = keep.tile([P, S2 // 16], U16, name="idx2")
@@ -128,54 +125,73 @@ def tile_list_neighbour_crop_scores_kernel(tc, tab_words, tab_scales, offs, offs
             prox_t[h] = stage.tile([P, PACK, HALF], F32, name="big")
             nc.sync.dma_start(prox_t[h][:], prox.rearrange("(u p) j -> p u j", p=P)[:, :, HALF * h : HALF * (h + 1)])
 
+        th = {}
         hb = {}
         hc = {}
         hs = {}
 
-        def features(b, c):
-            n = CHUNKS[c]
-            th = ring.tile([P, n, PACK], F32, name="th")
-            j0 = sum(CHUNKS[:c])
-            for i in range(n // UN):
-                js = slice(j0 + UN * i, j0 + UN * (i + 1))
-                acc = psum.tile([P, PACK, UN], F32, name="acc")
-                for t in range(PACK):
-                    m0 = P * t
-                    nc.tensor.matmul_mx(
-                        acc[:, t, :],
-                        lhsT=w1c[b][:, m0 : m0 + P].bitcast(FP8X4),
-                        lhsT_scale=w1s[b][:, m0 : m0 + P],
-                        rhs=vw[0][:, js].bitcast(FP8X4),
-                        rhs_scale=vs[ROW0[0] : P, js],
-                        start=True,
-                        stop=False,
-                    )
-                    r0 = KP * b + m0
-                    nc.tensor.matmul_mx(
-                        acc[:, t, :],
-                        lhsT=w4c[:, 2 * r0 : 2 * (r0 + P)].bitcast(FP4X4),
-                        lhsT_scale=w4s[:, r0 : r0 + P],
-                        rhs=vw[1][:, js].bitcast(FP8X4),
-                        rhs_scale=vs[ROW0[1] : P, js],
-                        start=False,
-                        stop=True,
-                    )
-                nc.scalar.activation(th[:, UN * i : UN * (i + 1), :], acc[:].rearrange("p t n -> p n t"), ACT.Tanh, bias=zero_bias[:])
-            hb[b, c] = ring.tile([P, n, PACK], BF16, name="hb", align_bytes=64)
-            nc.vector.tensor_tensor(hb[b, c][:], th[:], gain_t[:, b, :].unsqueeze(1).to_broadcast([P, n, PACK]), ALU.mult)
+        def features(b, h):
+            th[b, h] = keep.tile([P, PACK, HALF], F32, name="th%d%d" % (b, h))
+            js = slice(HALF * h, HALF * (h + 1))
+            for t in range(PACK):
+                acc = psum.tile([P, HALF], F32, name="acc", tag="bank")
+                m0 = P * t
+                nc.tensor.matmul_mx(
+                    acc[:],
+                    lhsT=w1c[b][:, m0 : m0 + P].bitcast(FP8X4),
+                    lhsT_scale=w1s[b][:, m0 : m0 + P],
+                    rhs=vw[0][:, js].bitcast(FP8X4),
+                    rhs_scale=vs[ROW0[0] : P, js],
+                    start=True,
+                    stop=False,
+                )
+                r0 = KP * b + m0
+                nc.tensor.matmul_mx(
+                    acc[:],
+                    lhsT=w4c[:, 2 * r0 : 2 * (r0 + P)].bitcast(FP4X4),
+                    lhsT_scale=w4s[:, r0 : r0 + P],
+                    rhs=vw[1][:, js].bitcast(FP8X4),
+                    rhs_scale=vs[ROW0[1] : P, js],
+                    start=False,
+                    stop=True,
+                )
+                nc.scalar.activation(th[b, h][:, t, :], acc[:], ACT.Tanh, bias=zero_bias[:])
 
-        def quantise_h(b, c):
-            n = CHUNKS[c]
-            hc[b, c] = keep.tile([P, n], U32, name="hc%d%d" % (b, c), align_bytes=64)
-            hs[b, c] = keep.tile([P, n], U8, name="hs%d%d" % (b, c), align_bytes=64)
-            nc.vector.quantize_mx(hc[b, c][:].bitcast(FP8X4), hs[b, c][:], hb[b, c][:].rearrange("p n t -> p (n t)"))
+        def gain_on_vector(b, start, n):
+            h, j0 = divmod(start, HALF)
+            hb[b, start] = keep.tile([P, PACK * n], BF16, name="hb%d_%d" % (b, start), align_bytes=64)
+            nc.vector.tensor_tensor(
+                hb[b, start][:].rearrange("p (c i t) -> p c t i", i=2, t=PACK),
+                th[b, h][:, :, j0 : j0 + n].rearrange("p t (c i) -> p c t i", i=2),
+                gain_t[:, b, :].unsqueeze(1).unsqueeze(3).to_broadcast([P, n // 2, PACK, 2]),
+                ALU.mult,
+            )
 
-        def scores(c):
-            n = CHUNKS[c]
-            start = sum(CHUNKS[:c])
+        def gain_on_scalar(b, h):
+            scaled = keep.tile([P, PACK, HALF], BF16, name="scaled")
+            for t in range(PACK):
+                nc.scalar.activation(scaled[:, t, :], th[b, h][:, t, :], ACT.Copy, scale=gain_t[:, b, t : t + 1])
+            return scaled
+
+        def interleave(scaled, b, start, n):
+            j0 = start % HALF
+            hb[b, start] = keep.tile([P, PACK * n], BF16, name="hb%d_%d" % (b, start), align_bytes=64)
+            nc.vector.tensor_copy(
+                hb[b, start][:].rearrange("p (c i t) -> p c t i", i=4, t=PACK),
+                scaled[:, :, j0 : j0 + n].rearrange("p t (c i) -> p c t i", i=4),
+            )
+
+        def quantise_h(b, start, n):
+            nc.vector.quantize_mx(hc[b][:, start : start + n].bitcast(FP8X4), hs[b][:, start : start + n], hb[b, start][:])
+
+        for b in range(2):
+            hc[b] = keep.tile([P, S], U32, name="hc%d" % b, align_bytes=64)
+            hs[b] = keep.tile([P, S], U8, name="hs%d" % b, align_bytes=64)
+
+        def scores(start, n):
             h, j0 = divmod(start, HALF)
             for u0 in range(0, PACK, 2):
-                e = psum.tile([P, 2, n], F32, name="e")
+                e = psum.tile([P, 2, n], F32, name="e", tag="bank")
                 for u in range(u0, u0 + 2):
                     ms = slice(P * u, P * (u + 1))
                     for a in range(2):
@@ -183,16 +199,16 @@ def tile_list_neighbour_crop_scores_kernel(tc, tab_words, tab_scales, offs, offs
                             e[:, u - u0, :],
                             lhsT=v2w[a][:, ms].bitcast(FP8X4),
                             lhsT_scale=v2s[ROW0[a] : P, ms],
-                            rhs=hc[a, c][:].bitcast(FP8X4),
-                            rhs_scale=hs[a, c][:],
+                            rhs=hc[a][:, start : start + n].bitcast(FP8X4),
+                            rhs_scale=hs[a][:, start : start + n],
                             start=(a == 0),
                             stop=(a == 1),
                         )
-                pe = ring.tile([P, 2, n], F32, name="pe")
-                res = ring.tile([P, 2, n], F32, name="res")
+                pe = keep.tile([P, 2, n], F32, name="pe%d_%d" % (start, u0))
+                res = keep.tile([P, 2, n], F32, name="res%d_%d" % (start, u0))
                 nc.vector.tensor_tensor(pe[:], e[:], prox_t[h][:, u0 : u0 + 2, j0 : j0 + n], ALU.mult)
                 for u in range(u0, u0 + 2):
-                    if c == len(CHUNKS) - 1 and u == PACK - 1:
+                    if start + n == S and u == PACK - 1:
                         nc.vector.tensor_scalar(res[:, u - u0, :], pe[:, u - u0, :], base_t[:, u : u + 1], None, ALU.add)
                     else:
                         nc.scalar.activation(res[:, u - u0, :], pe[:, u - u0, :], ACT.Identity, bias=base_t[:, u : u + 1])
@@ -204,15 +220,27 @@ def tile_list_neighbour_crop_scores_kernel(tc, tab_words, tab_scales, offs, offs
         v2w[0] = gather("v2w0", wins[0], U32, idx2[:])
         load_prox(0)
         load_prox(1)
-        last = len(CHUNKS) - 1
-        for c in range(len(CHUNKS)):
-            features(0, c)
-            if c > 0:
-                quantise_h(1, c - 1)
-            features(1, c)
-            quantise_h(0, c)
-            if 0 < c < last:
-                scores(c - 1)
-        quantise_h(1, last)
-        scores(last - 1)
-        scores(last)
+        features(0, 0)
+        features(1, 0)
+        features(0, 1)
+        features(1, 1)
+        scaled = gain_on_scalar(1, 1)
+        gain_on_vector(0, 0, 512)
+        gain_on_vector(1, 0, 256)
+        quantise_h(0, 0, 512)
+        gain_on_vector(1, 256, 256)
+        quantise_h(1, 0, 256)
+        gain_on_vector(0, 512, 512)
+        quantise_h(1, 256, 256)
+        scores(0, 256)
+        quantise_h(0, 512, 512)
+        interleave(scaled, 1, 512, 256)
+        scores(256, 256)
+        quantise_h(1, 512, 256)
+        interleave(scaled, 1, 768, 128)
+        interleave(scaled, 1, 896, 128)
+        quantise_h(1, 768, 128)
+        scores(512, 256)
+        quantise_h(1, 896, 128)
+        scores(768, 128)
+        scores(896, 128)

@@ -19,8 +19,14 @@ ALU = mybir.AluOpType
 P = 128
 PACK = 4
 KP = P * PACK
+PASSES = K // KP
+BLOCKS = KP // 32
+M_TILES = S2 // P
 HALF = S // 2
-ROW0 = (4, 0)
+QUARTER = S // 4
+EIGHTH = S // 8
+SCALE_ROW = (4, 0)
+EARLY_SCALE_LOADS = 5
 
 
 def tile_list_neighbour_crop_scores_kernel(tc, tab_words, tab_scales, offs, offs2, w1, w4_words, w4_scales, gain, prox, base, out):
@@ -32,215 +38,217 @@ def tile_list_neighbour_crop_scores_kernel(tc, tab_words, tab_scales, offs, offs
 
         idx = keep.tile([P, S // 16], U16, name="idx")
         idx2 = keep.tile([P, S2 // 16], U16, name="idx2")
-        tw = [keep.tile([P, T], I32, name="tw%d" % a, align_bytes=64) for a in range(2)]
-        ts = keep.tile([P, T], U8, name="ts", align_bytes=64)
-        w4raw = keep.tile([P, 2 * K], U8, name="w4raw", align_bytes=64)
-        w4sraw = keep.tile([P, K], U8, name="w4sraw", align_bytes=64)
-        gain_t = keep.tile([P, 2, PACK], F32, name="gain_t")
-        base_t = keep.tile([P, PACK], F32, name="base_t")
+        table = [keep.tile([P, T], I32, name="table%d" % a, align_bytes=64) for a in range(PASSES)]
+        table_scales = keep.tile([P, T], U8, name="table_scales", align_bytes=64)
+        w4_raw = keep.tile([P, 2 * K], U8, name="w4_raw", align_bytes=64)
+        w4_raw_scales = keep.tile([P, K], U8, name="w4_raw_scales", align_bytes=64)
+        gain_t = keep.tile([P, PASSES, PACK], F32, name="gain_t")
+        base_t = keep.tile([P, M_TILES], F32, name="base_t")
         zero = keep.tile([P, 1], F32, name="zero")
         zero_bias = keep.tile([P, 1], F32, name="zero_bias")
 
-        nc.vector.memset(ts[:].bitcast(I32), 0)
+        nc.vector.memset(table_scales[:].bitcast(I32), 0)
         nc.vector.memset(zero[:], 0.0)
-        nc.vector.memset(w4sraw[:].bitcast(I32), 0)
+        nc.vector.memset(w4_raw_scales[:].bitcast(I32), 0)
 
-        def load_words(a):
-            nc.sync.dma_start(tw[a][:], tab_words[a].rearrange("p t i -> p (t i)").bitcast(I32))
+        def load_table(a):
+            nc.sync.dma_start(table[a][:], tab_words[a].rearrange("p t i -> p (t i)").bitcast(I32))
+
+        def load_table_scales(n):
+            r, a = divmod(n, PASSES)
+            nc.sync.dma_start(table_scales[SCALE_ROW[a] + r : P : 32, :].bitcast(I32), tab_scales[a, r:BLOCKS:4, :].bitcast(I32))
+
+        def load_w4_scales(r):
+            nc.sync.dma_start(w4_raw_scales[r:P:32, :].bitcast(I32), w4_scales[0, r:BLOCKS:4, :].bitcast(I32))
 
         def load_w1(b):
-            raw = stage.tile([P, PACK, KP], F32, name="big")
-            nc.sync.dma_start(raw[:], w1.rearrange("(p j) c -> p j c", j=PACK)[:, :, KP * b : KP * (b + 1)])
+            raw = stage.tile([P, PACK, KP], F32, name="wide")
+            nc.sync.dma_start(raw[:], w1.rearrange("(p i) c -> p i c", i=PACK)[:, :, KP * b : KP * (b + 1)])
             return raw
 
-        def load_scales(n):
-            a, q = divmod(n, 4)
-            r = 32 * q + ROW0[a]
-            nc.sync.dma_start(ts[r : r + 4, :].bitcast(I32), tab_scales[a, 4 * q : 4 * q + 4, :].bitcast(I32))
-
-        def load_w4_scales(q):
-            nc.sync.dma_start(w4sraw[32 * q : 32 * q + 4, :].bitcast(I32), w4_scales[0, 4 * q : 4 * q + 4, :].bitcast(I32))
-
         nc.sync.dma_start(idx[:], offs)
-        load_words(1)
-        for n in range(5):
-            load_scales(n)
-        load_words(0)
-        for n in range(5, 8):
-            load_scales(n)
-        w1raw = [load_w1(0)]
-        nc.sync.dma_start(w4raw[:].bitcast(I32), w4_words[0].bitcast(I32))
-        for q in range(3):
-            load_w4_scales(q)
-        w1raw.append(load_w1(1))
+        load_table(1)
+        for n in range(EARLY_SCALE_LOADS):
+            load_table_scales(n)
+        load_table(0)
+        for n in range(EARLY_SCALE_LOADS, 4 * PASSES):
+            load_table_scales(n)
+        w1_raw = [load_w1(0)]
+        load_w4_scales(0)
+        load_w4_scales(1)
+        w1_raw.append(load_w1(1))
+        nc.sync.dma_start(w4_raw[:].bitcast(I32), w4_words[0].bitcast(I32))
+        load_w4_scales(2)
         load_w4_scales(3)
         nc.sync.dma_start(idx2[:], offs2)
-        nc.sync.dma_start(gain_t[:], gain.rearrange("(b p t) -> p b t", b=2, t=PACK))
+        nc.sync.dma_start(gain_t[:], gain.rearrange("(b p t) -> p b t", b=PASSES, t=PACK))
         with nc.allow_non_contiguous_dma(reason="one offset for each output row"):
             nc.sync.dma_start(base_t[:], base.rearrange("(u p) -> p u", p=P))
         nc.scalar.activation(zero_bias[:], zero[:], ACT.Tanh)
 
         def gather(name, window, dtype, offsets):
-            n = 16 * offsets.shape[1]
-            g = keep.tile([P, n], dtype, name=name, align_bytes=64)
-            nc.vector.tensor_copy(g[:], window.indirect(offsets))
-            return g
+            picked = keep.tile([P, 16 * offsets.shape[1]], dtype, name=name, align_bytes=64)
+            nc.vector.tensor_copy(picked[:], window.indirect(offsets))
+            return picked
 
-        wins = [tw[a][:].bitcast(U32) for a in range(2)]
-        vw = {}
-        v2w = {}
-        vw[1] = gather("vw1", wins[1], U32, idx[:])
-        vw[0] = gather("vw0", wins[0], U32, idx[:])
-        vs = gather("vs", ts[:], U8, idx[:])
+        table_u32 = [table[a][:].bitcast(U32) for a in range(PASSES)]
+        cand = {}
+        cand[1] = gather("cand1", table_u32[1], U32, idx[:])
+        cand[0] = gather("cand0", table_u32[0], U32, idx[:])
+        cand_scales = gather("cand_scales", table_scales[:], U8, idx[:])
 
-        w1c = {}
-        w1s = {}
+        w1_codes = {}
+        w1_scales = {}
 
         def quantise_w1(b):
-            wb = stage.tile([P, KP * PACK], BF16, name="wb", align_bytes=64)
+            rounded = stage.tile([P, KP * PACK], BF16, name="w1_rounded", align_bytes=64)
             nc.scalar.copy(
-                wb[:].rearrange("p (th tl m j) -> p th m j tl", th=2, tl=2, j=PACK),
-                w1raw[b][:].rearrange("p j (m th tl) -> p th m j tl", th=2, tl=2),
+                rounded[:].rearrange("p (th tl m i) -> p th m i tl", th=2, tl=2, i=PACK),
+                w1_raw[b][:].rearrange("p i (m th tl) -> p th m i tl", th=2, tl=2),
             )
-            w1c[b] = keep.tile([P, KP], U32, name="w1c%d" % b, align_bytes=64)
-            w1s[b] = keep.tile([P, KP], U8, name="w1s%d" % b, align_bytes=64)
-            nc.vector.quantize_mx(w1c[b][:].bitcast(FP8X4), w1s[b][:], wb[:])
+            w1_codes[b] = keep.tile([P, KP], U32, name="w1_codes%d" % b, align_bytes=64)
+            w1_scales[b] = keep.tile([P, KP], U8, name="w1_scales%d" % b, align_bytes=64)
+            nc.vector.quantize_mx(w1_codes[b][:].bitcast(FP8X4), w1_scales[b][:], rounded[:])
 
-
-        w4c = keep.tile([P, 2 * K], U8, name="w4c", align_bytes=64)
-        w4s = keep.tile([P, K], U8, name="w4s", align_bytes=64)
-        nc.vector.tensor_copy(
-            w4c[:].bitcast(U16).rearrange("p (b t m) -> p b t m", b=2, t=PACK),
-            w4raw[:].bitcast(U16).rearrange("p (b m t) -> p b t m", b=2, t=PACK),
-        )
         quantise_w1(0)
+        w4_codes = keep.tile([P, 2 * K], U8, name="w4_codes", align_bytes=64)
+        w4_scales_t = keep.tile([P, K], U8, name="w4_scales_t", align_bytes=64)
         nc.vector.tensor_copy(
-            w4s[:].rearrange("p (b t m) -> p b t m", b=2, t=PACK),
-            w4sraw[:].rearrange("p (b m t) -> p b t m", b=2, t=PACK),
+            w4_codes[:].bitcast(U16).rearrange("p (b t m) -> p b t m", b=PASSES, t=PACK),
+            w4_raw[:].bitcast(U16).rearrange("p (b m t) -> p b t m", b=PASSES, t=PACK),
         )
+        nc.vector.tensor_copy(
+            w4_scales_t[:].rearrange("p (b t m) -> p b t m", b=PASSES, t=PACK),
+            w4_raw_scales[:].rearrange("p (b m t) -> p b t m", b=PASSES, t=PACK),
+        )
+        h_codes = {}
+        h_scales = {}
+        for b in range(PASSES):
+            h_codes[b] = keep.tile([P, S], U32, name="h_codes%d" % b, align_bytes=64)
+            h_scales[b] = keep.tile([P, S], U8, name="h_scales%d" % b, align_bytes=64)
+        quantise_w1(1)
 
+        sown_scales = gather("sown_scales", table_scales[:], U8, idx2[:])
+        sown = {}
+        sown[1] = gather("sown1", table_u32[1], U32, idx2[:])
+        sown[0] = gather("sown0", table_u32[0], U32, idx2[:])
         prox_t = {}
+        for half in range(2):
+            prox_t[half] = stage.tile([P, M_TILES, HALF], F32, name="wide")
+            nc.sync.dma_start(prox_t[half][:], prox.rearrange("(u p) j -> p u j", p=P)[:, :, HALF * half : HALF * (half + 1)])
 
-        def load_prox(h):
-            prox_t[h] = stage.tile([P, PACK, HALF], F32, name="big")
-            nc.sync.dma_start(prox_t[h][:], prox.rearrange("(u p) j -> p u j", p=P)[:, :, HALF * h : HALF * (h + 1)])
+        tanh_t = {}
+        h_scaled = {}
+        h_rounded = {}
 
-        th = {}
-        hb = {}
-        hc = {}
-        hs = {}
-
-        def features(b, h):
-            th[b, h] = keep.tile([P, PACK, HALF], F32, name="th%d%d" % (b, h))
-            js = slice(HALF * h, HALF * (h + 1))
+        def features(b, half):
+            tanh_t[b, half] = keep.tile([P, PACK, HALF], F32, name="tanh%d%d" % (b, half))
+            js = slice(HALF * half, HALF * (half + 1))
             for t in range(PACK):
                 acc = psum.tile([P, HALF], F32, name="acc", tag="bank")
-                m0 = P * t
+                c0 = P * t
                 nc.tensor.matmul_mx(
                     acc[:],
-                    lhsT=w1c[b][:, m0 : m0 + P].bitcast(FP8X4),
-                    lhsT_scale=w1s[b][:, m0 : m0 + P],
-                    rhs=vw[0][:, js].bitcast(FP8X4),
-                    rhs_scale=vs[ROW0[0] : P, js],
+                    lhsT=w1_codes[b][:, c0 : c0 + P].bitcast(FP8X4),
+                    lhsT_scale=w1_scales[b][:, c0 : c0 + P],
+                    rhs=cand[0][:, js].bitcast(FP8X4),
+                    rhs_scale=cand_scales[SCALE_ROW[0] : P, js],
                     start=True,
                     stop=False,
                 )
-                r0 = KP * b + m0
+                c1 = KP * b + c0
                 nc.tensor.matmul_mx(
                     acc[:],
-                    lhsT=w4c[:, 2 * r0 : 2 * (r0 + P)].bitcast(FP4X4),
-                    lhsT_scale=w4s[:, r0 : r0 + P],
-                    rhs=vw[1][:, js].bitcast(FP8X4),
-                    rhs_scale=vs[ROW0[1] : P, js],
+                    lhsT=w4_codes[:, 2 * c1 : 2 * (c1 + P)].bitcast(FP4X4),
+                    lhsT_scale=w4_scales_t[:, c1 : c1 + P],
+                    rhs=cand[1][:, js].bitcast(FP8X4),
+                    rhs_scale=cand_scales[SCALE_ROW[1] : P, js],
                     start=False,
                     stop=True,
                 )
-                nc.scalar.activation(th[b, h][:, t, :], acc[:], ACT.Tanh, bias=zero_bias[:])
+                nc.scalar.activation(tanh_t[b, half][:, t, :], acc[:], ACT.Tanh, bias=zero_bias[:])
 
         def gain_on_vector(b, start, n):
-            h, j0 = divmod(start, HALF)
-            hb[b, start] = keep.tile([P, PACK * n], BF16, name="hb%d_%d" % (b, start), align_bytes=64)
+            half, j0 = divmod(start, HALF)
+            h_rounded[b, start] = keep.tile([P, PACK * n], BF16, name="h_rounded%d_%d" % (b, start), align_bytes=64)
             nc.vector.tensor_tensor(
-                hb[b, start][:].rearrange("p (c i t) -> p c t i", i=2, t=PACK),
-                th[b, h][:, :, j0 : j0 + n].rearrange("p t (c i) -> p c t i", i=2),
+                h_rounded[b, start][:].rearrange("p (c i t) -> p c t i", i=2, t=PACK),
+                tanh_t[b, half][:, :, j0 : j0 + n].rearrange("p t (c i) -> p c t i", i=2),
                 gain_t[:, b, :].unsqueeze(1).unsqueeze(3).to_broadcast([P, n // 2, PACK, 2]),
                 ALU.mult,
             )
 
-        def gain_on_scalar(b, h):
-            scaled = keep.tile([P, PACK, HALF], BF16, name="scaled")
+        def gain_on_scalar(b, start):
+            half, j0 = divmod(start, HALF)
+            scaled = keep.tile([P, PACK, QUARTER], BF16, name="scaled%d_%d" % (b, start))
             for t in range(PACK):
-                nc.scalar.activation(scaled[:, t, :], th[b, h][:, t, :], ACT.Copy, scale=gain_t[:, b, t : t + 1])
-            return scaled
+                nc.scalar.activation(scaled[:, t, :], tanh_t[b, half][:, t, j0 : j0 + QUARTER], ACT.Copy, scale=gain_t[:, b, t : t + 1])
+            h_scaled[b, start // QUARTER] = scaled
 
-        def interleave(scaled, b, start, n):
-            j0 = start % HALF
-            hb[b, start] = keep.tile([P, PACK * n], BF16, name="hb%d_%d" % (b, start), align_bytes=64)
+        def interleave(b, start, n):
+            quarter, j0 = divmod(start, QUARTER)
+            h_rounded[b, start] = keep.tile([P, PACK * n], BF16, name="h_rounded%d_%d" % (b, start), align_bytes=64)
             nc.vector.tensor_copy(
-                hb[b, start][:].rearrange("p (c i t) -> p c t i", i=4, t=PACK),
-                scaled[:, :, j0 : j0 + n].rearrange("p t (c i) -> p c t i", i=4),
+                h_rounded[b, start][:].rearrange("p (c i t) -> p c t i", i=4, t=PACK),
+                h_scaled[b, quarter][:, :, j0 : j0 + n].rearrange("p t (c i) -> p c t i", i=4),
             )
 
         def quantise_h(b, start, n):
-            nc.vector.quantize_mx(hc[b][:, start : start + n].bitcast(FP8X4), hs[b][:, start : start + n], hb[b, start][:])
-
-        for b in range(2):
-            hc[b] = keep.tile([P, S], U32, name="hc%d" % b, align_bytes=64)
-            hs[b] = keep.tile([P, S], U8, name="hs%d" % b, align_bytes=64)
+            nc.vector.quantize_mx(h_codes[b][:, start : start + n].bitcast(FP8X4), h_scales[b][:, start : start + n], h_rounded[b, start][:])
 
         def scores(start, n):
-            h, j0 = divmod(start, HALF)
-            for u0 in range(0, PACK, 2):
+            half, j0 = divmod(start, HALF)
+            for u0 in range(0, M_TILES, 2):
                 e = psum.tile([P, 2, n], F32, name="e", tag="bank")
                 for u in range(u0, u0 + 2):
                     ms = slice(P * u, P * (u + 1))
-                    for a in range(2):
+                    for a in range(PASSES):
                         nc.tensor.matmul_mx(
                             e[:, u - u0, :],
-                            lhsT=v2w[a][:, ms].bitcast(FP8X4),
-                            lhsT_scale=v2s[ROW0[a] : P, ms],
-                            rhs=hc[a][:, start : start + n].bitcast(FP8X4),
-                            rhs_scale=hs[a][:, start : start + n],
+                            lhsT=sown[a][:, ms].bitcast(FP8X4),
+                            lhsT_scale=sown_scales[SCALE_ROW[a] : P, ms],
+                            rhs=h_codes[a][:, start : start + n].bitcast(FP8X4),
+                            rhs_scale=h_scales[a][:, start : start + n],
                             start=(a == 0),
-                            stop=(a == 1),
+                            stop=(a == PASSES - 1),
                         )
-                pe = keep.tile([P, 2, n], F32, name="pe%d_%d" % (start, u0))
-                res = keep.tile([P, 2, n], F32, name="res%d_%d" % (start, u0))
-                nc.vector.tensor_tensor(pe[:], e[:], prox_t[h][:, u0 : u0 + 2, j0 : j0 + n], ALU.mult)
+                weighted = keep.tile([P, 2, n], F32, name="weighted%d_%d" % (start, u0))
+                result = keep.tile([P, 2, n], F32, name="result%d_%d" % (start, u0))
+                nc.vector.tensor_tensor(weighted[:], e[:], prox_t[half][:, u0 : u0 + 2, j0 : j0 + n], ALU.mult)
                 for u in range(u0, u0 + 2):
-                    if start + n == S and u == PACK - 1:
-                        nc.vector.tensor_scalar(res[:, u - u0, :], pe[:, u - u0, :], base_t[:, u : u + 1], None, ALU.add)
+                    if start + n == S and u == M_TILES - 1:
+                        nc.vector.tensor_scalar(result[:, u - u0, :], weighted[:, u - u0, :], base_t[:, u : u + 1], None, ALU.add)
                     else:
-                        nc.scalar.activation(res[:, u - u0, :], pe[:, u - u0, :], ACT.Identity, bias=base_t[:, u : u + 1])
-                nc.sync.dma_start(out.rearrange("(u p) j -> p u j", p=P)[:, u0 : u0 + 2, start : start + n], res[:])
+                        nc.scalar.activation(result[:, u - u0, :], weighted[:, u - u0, :], ACT.Identity, bias=base_t[:, u : u + 1])
+                nc.sync.dma_start(out.rearrange("(u p) j -> p u j", p=P)[:, u0 : u0 + 2, start : start + n], result[:])
 
-        quantise_w1(1)
-        v2s = gather("v2s", ts[:], U8, idx2[:])
-        v2w[1] = gather("v2w1", wins[1], U32, idx2[:])
-        v2w[0] = gather("v2w0", wins[0], U32, idx2[:])
-        load_prox(0)
-        load_prox(1)
-        features(0, 0)
-        features(1, 0)
-        features(0, 1)
-        features(1, 1)
-        scaled = gain_on_scalar(1, 1)
-        gain_on_vector(0, 0, 512)
-        gain_on_vector(1, 0, 256)
-        quantise_h(0, 0, 512)
-        gain_on_vector(1, 256, 256)
-        quantise_h(1, 0, 256)
-        gain_on_vector(0, 512, 512)
-        quantise_h(1, 256, 256)
-        scores(0, 256)
-        quantise_h(0, 512, 512)
-        interleave(scaled, 1, 512, 256)
-        scores(256, 256)
-        quantise_h(1, 512, 256)
-        interleave(scaled, 1, 768, 128)
-        interleave(scaled, 1, 896, 128)
-        quantise_h(1, 768, 128)
-        scores(512, 256)
-        quantise_h(1, 896, 128)
-        scores(768, 128)
-        scores(896, 128)
+        for half in range(2):
+            for b in range(PASSES):
+                features(b, half)
+        last_quarter = S - QUARTER
+        last_eighth = S - EIGHTH
+        gain_on_scalar(1, HALF)
+        gain_on_scalar(0, last_quarter)
+        gain_on_scalar(1, last_quarter)
+
+        gain_on_vector(0, 0, HALF)
+        gain_on_vector(1, 0, QUARTER)
+        quantise_h(0, 0, HALF)
+        gain_on_vector(1, QUARTER, QUARTER)
+        quantise_h(1, 0, QUARTER)
+        gain_on_vector(0, HALF, QUARTER)
+        quantise_h(1, QUARTER, QUARTER)
+        scores(0, QUARTER)
+        quantise_h(0, HALF, QUARTER)
+        interleave(1, HALF, QUARTER)
+        scores(QUARTER, QUARTER)
+        quantise_h(1, HALF, QUARTER)
+        interleave(0, last_quarter, QUARTER)
+        interleave(1, last_quarter, EIGHTH)
+        quantise_h(0, last_quarter, QUARTER)
+        interleave(1, last_eighth, EIGHTH)
+        quantise_h(1, last_quarter, EIGHTH)
+        scores(HALF, QUARTER)
+        quantise_h(1, last_eighth, EIGHTH)
+        scores(last_quarter, EIGHTH)
+        scores(last_eighth, EIGHTH)

from contextlib import ExitStack

import concourse.mybir as mybir

K, T, S, S2 = 1024, 2048, 1024, 512
FLOPS = 2 * K * K * S + 2 * K * S2 * S

F32 = mybir.dt.float32
BF16 = mybir.dt.bfloat16
I32 = mybir.dt.int32
U32 = mybir.dt.uint32
U16 = mybir.dt.uint16
U8 = mybir.dt.uint8
FP8X4 = mybir.dt.float8_e4m3fn_x4
FP4X4 = mybir.dt.float4_e2m1fn_x4
ACT = mybir.ActivationFunctionType
ALU = mybir.AluOpType

P = 128
PACK = 4
KP = P * PACK
PASSES = K // KP
BLOCKS = KP // 32
M_TILES = S2 // P
HALF = S // 2
QUARTER = S // 4
EIGHTH = S // 8
SCALE_ROW = (4, 0)
EARLY_SCALE_LOADS = 5


def tile_list_neighbour_crop_scores_kernel(tc, tab_words, tab_scales, offs, offs2, w1, w4_words, w4_scales, gain, prox, base, out):
    nc = tc.nc
    with ExitStack() as ctx:
        keep = ctx.enter_context(tc.tile_pool(name="keep", bufs=1))
        stage = ctx.enter_context(tc.tile_pool(name="stage", bufs=2))
        psum = ctx.enter_context(tc.psum_pool(name="psum", bufs=8))

        idx = keep.tile([P, S // 16], U16, name="idx")
        idx2 = keep.tile([P, S2 // 16], U16, name="idx2")
        table = [keep.tile([P, T], I32, name="table%d" % a, align_bytes=64) for a in range(PASSES)]
        table_scales = keep.tile([P, T], U8, name="table_scales", align_bytes=64)
        w4_raw = keep.tile([P, 2 * K], U8, name="w4_raw", align_bytes=64)
        w4_raw_scales = keep.tile([P, K], U8, name="w4_raw_scales", align_bytes=64)
        gain_t = keep.tile([P, PASSES, PACK], F32, name="gain_t")
        base_t = keep.tile([P, M_TILES], F32, name="base_t")
        zero = keep.tile([P, 1], F32, name="zero")
        zero_bias = keep.tile([P, 1], F32, name="zero_bias")

        nc.vector.memset(table_scales[:].bitcast(I32), 0)
        nc.vector.memset(zero[:], 0.0)
        nc.vector.memset(w4_raw_scales[:].bitcast(I32), 0)

        def load_table(a):
            nc.sync.dma_start(table[a][:], tab_words[a].rearrange("p t i -> p (t i)").bitcast(I32))

        def load_table_scales(n):
            r, a = divmod(n, PASSES)
            nc.sync.dma_start(table_scales[SCALE_ROW[a] + r : P : 32, :].bitcast(I32), tab_scales[a, r:BLOCKS:4, :].bitcast(I32))

        def load_w4_scales(r):
            nc.sync.dma_start(w4_raw_scales[r:P:32, :].bitcast(I32), w4_scales[0, r:BLOCKS:4, :].bitcast(I32))

        def load_w1(b):
            raw = stage.tile([P, PACK, KP], F32, name="wide")
            nc.sync.dma_start(raw[:], w1.rearrange("(p i) c -> p i c", i=PACK)[:, :, KP * b : KP * (b + 1)])
            return raw

        nc.sync.dma_start(idx[:], offs)
        load_table(1)
        for n in range(EARLY_SCALE_LOADS):
            load_table_scales(n)
        load_table(0)
        for n in range(EARLY_SCALE_LOADS, 4 * PASSES):
            load_table_scales(n)
        w1_raw = [load_w1(0)]
        load_w4_scales(0)
        load_w4_scales(1)
        w1_raw.append(load_w1(1))
        nc.sync.dma_start(w4_raw[:].bitcast(I32), w4_words[0].bitcast(I32))
        load_w4_scales(2)
        load_w4_scales(3)
        nc.sync.dma_start(idx2[:], offs2)
        nc.sync.dma_start(gain_t[:], gain.rearrange("(b p t) -> p b t", b=PASSES, t=PACK))
        with nc.allow_non_contiguous_dma(reason="one offset for each output row"):
            nc.sync.dma_start(base_t[:], base.rearrange("(u p) -> p u", p=P))
        nc.scalar.activation(zero_bias[:], zero[:], ACT.Tanh)

        def gather(name, window, dtype, offsets):
            picked = keep.tile([P, 16 * offsets.shape[1]], dtype, name=name, align_bytes=64)
            nc.vector.tensor_copy(picked[:], window.indirect(offsets))
            return picked

        table_u32 = [table[a][:].bitcast(U32) for a in range(PASSES)]
        cand = {}
        cand[1] = gather("cand1", table_u32[1], U32, idx[:])
        cand[0] = gather("cand0", table_u32[0], U32, idx[:])
        cand_scales = gather("cand_scales", table_scales[:], U8, idx[:])

        w1_codes = {}
        w1_scales = {}

        def quantise_w1(b):
            rounded = stage.tile([P, KP * PACK], BF16, name="w1_rounded", align_bytes=64)
            nc.scalar.copy(
                rounded[:].rearrange("p (th tl m i) -> p th m i tl", th=2, tl=2, i=PACK),
                w1_raw[b][:].rearrange("p i (m th tl) -> p th m i tl", th=2, tl=2),
            )
            w1_codes[b] = keep.tile([P, KP], U32, name="w1_codes%d" % b, align_bytes=64)
            w1_scales[b] = keep.tile([P, KP], U8, name="w1_scales%d" % b, align_bytes=64)
            nc.vector.quantize_mx(w1_codes[b][:].bitcast(FP8X4), w1_scales[b][:], rounded[:])

        quantise_w1(0)
        w4_codes = keep.tile([P, 2 * K], U8, name="w4_codes", align_bytes=64)
        w4_scales_t = keep.tile([P, K], U8, name="w4_scales_t", align_bytes=64)
        nc.vector.tensor_copy(
            w4_codes[:].bitcast(U16).rearrange("p (b t m) -> p b t m", b=PASSES, t=PACK),
            w4_raw[:].bitcast(U16).rearrange("p (b m t) -> p b t m", b=PASSES, t=PACK),
        )
        nc.vector.tensor_copy(
            w4_scales_t[:].rearrange("p (b t m) -> p b t m", b=PASSES, t=PACK),
            w4_raw_scales[:].rearrange("p (b m t) -> p b t m", b=PASSES, t=PACK),
        )
        h_codes = {}
        h_scales = {}
        for b in range(PASSES):
            h_codes[b] = keep.tile([P, S], U32, name="h_codes%d" % b, align_bytes=64)
            h_scales[b] = keep.tile([P, S], U8, name="h_scales%d" % b, align_bytes=64)
        quantise_w1(1)

        sown_scales = gather("sown_scales", table_scales[:], U8, idx2[:])
        sown = {}
        sown[1] = gather("sown1", table_u32[1], U32, idx2[:])
        sown[0] = gather("sown0", table_u32[0], U32, idx2[:])
        prox_t = {}
        for half in range(2):
            prox_t[half] = stage.tile([P, M_TILES, HALF], F32, name="wide")
            nc.sync.dma_start(prox_t[half][:], prox.rearrange("(u p) j -> p u j", p=P)[:, :, HALF * half : HALF * (half + 1)])

        tanh_t = {}
        h_scaled = {}
        h_rounded = {}

        def features(b, half):
            tanh_t[b, half] = keep.tile([P, PACK, HALF], F32, name="tanh%d%d" % (b, half))
            js = slice(HALF * half, HALF * (half + 1))
            for t in range(PACK):
                acc = psum.tile([P, HALF], F32, name="acc", tag="bank")
                c0 = P * t
                nc.tensor.matmul_mx(
                    acc[:],
                    lhsT=w1_codes[b][:, c0 : c0 + P].bitcast(FP8X4),
                    lhsT_scale=w1_scales[b][:, c0 : c0 + P],
                    rhs=cand[0][:, js].bitcast(FP8X4),
                    rhs_scale=cand_scales[SCALE_ROW[0] : P, js],
                    start=True,
                    stop=False,
                )
                c1 = KP * b + c0
                nc.tensor.matmul_mx(
                    acc[:],
                    lhsT=w4_codes[:, 2 * c1 : 2 * (c1 + P)].bitcast(FP4X4),
                    lhsT_scale=w4_scales_t[:, c1 : c1 + P],
                    rhs=cand[1][:, js].bitcast(FP8X4),
                    rhs_scale=cand_scales[SCALE_ROW[1] : P, js],
                    start=False,
                    stop=True,
                )
                nc.scalar.activation(tanh_t[b, half][:, t, :], acc[:], ACT.Tanh, bias=zero_bias[:])

        def gain_on_vector(b, start, n):
            half, j0 = divmod(start, HALF)
            h_rounded[b, start] = keep.tile([P, PACK * n], BF16, name="h_rounded%d_%d" % (b, start), align_bytes=64)
            nc.vector.tensor_tensor(
                h_rounded[b, start][:].rearrange("p (c i t) -> p c t i", i=2, t=PACK),
                tanh_t[b, half][:, :, j0 : j0 + n].rearrange("p t (c i) -> p c t i", i=2),
                gain_t[:, b, :].unsqueeze(1).unsqueeze(3).to_broadcast([P, n // 2, PACK, 2]),
                ALU.mult,
            )

        def gain_on_scalar(b, start):
            half, j0 = divmod(start, HALF)
            scaled = keep.tile([P, PACK, QUARTER], BF16, name="scaled%d_%d" % (b, start))
            for t in range(PACK):
                nc.scalar.activation(scaled[:, t, :], tanh_t[b, half][:, t, j0 : j0 + QUARTER], ACT.Copy, scale=gain_t[:, b, t : t + 1])
            h_scaled[b, start // QUARTER] = scaled

        def interleave(b, start, n):
            quarter, j0 = divmod(start, QUARTER)
            h_rounded[b, start] = keep.tile([P, PACK * n], BF16, name="h_rounded%d_%d" % (b, start), align_bytes=64)
            nc.vector.tensor_copy(
                h_rounded[b, start][:].rearrange("p (c i t) -> p c t i", i=4, t=PACK),
                h_scaled[b, quarter][:, :, j0 : j0 + n].rearrange("p t (c i) -> p c t i", i=4),
            )

        def quantise_h(b, start, n):
            nc.vector.quantize_mx(h_codes[b][:, start : start + n].bitcast(FP8X4), h_scales[b][:, start : start + n], h_rounded[b, start][:])

        def scores(start, n):
            half, j0 = divmod(start, HALF)
            for u0 in range(0, M_TILES, 2):
                e = psum.tile([P, 2, n], F32, name="e", tag="bank")
                for u in range(u0, u0 + 2):
                    ms = slice(P * u, P * (u + 1))
                    for a in range(PASSES):
                        nc.tensor.matmul_mx(
                            e[:, u - u0, :],
                            lhsT=sown[a][:, ms].bitcast(FP8X4),
                            lhsT_scale=sown_scales[SCALE_ROW[a] : P, ms],
                            rhs=h_codes[a][:, start : start + n].bitcast(FP8X4),
                            rhs_scale=h_scales[a][:, start : start + n],
                            start=(a == 0),
                            stop=(a == PASSES - 1),
                        )
                weighted = keep.tile([P, 2, n], F32, name="weighted%d_%d" % (start, u0))
                result = keep.tile([P, 2, n], F32, name="result%d_%d" % (start, u0))
                nc.vector.tensor_tensor(weighted[:], e[:], prox_t[half][:, u0 : u0 + 2, j0 : j0 + n], ALU.mult)
                for u in range(u0, u0 + 2):
                    if start + n == S and u == M_TILES - 1:
                        nc.vector.tensor_scalar(result[:, u - u0, :], weighted[:, u - u0, :], base_t[:, u : u + 1], None, ALU.add)
                    else:
                        nc.scalar.activation(result[:, u - u0, :], weighted[:, u - u0, :], ACT.Identity, bias=base_t[:, u : u + 1])
                nc.sync.dma_start(out.rearrange("(u p) j -> p u j", p=P)[:, u0 : u0 + 2, start : start + n], result[:])

        for half in range(2):
            for b in range(PASSES):
                features(b, half)
        last_quarter = S - QUARTER
        last_eighth = S - EIGHTH
        gain_on_scalar(1, HALF)
        gain_on_scalar(0, last_quarter)
        gain_on_scalar(1, last_quarter)

        gain_on_vector(0, 0, HALF)
        gain_on_vector(1, 0, QUARTER)
        quantise_h(0, 0, HALF)
        gain_on_vector(1, QUARTER, QUARTER)
        quantise_h(1, 0, QUARTER)
        gain_on_vector(0, HALF, QUARTER)
        quantise_h(1, QUARTER, QUARTER)
        scores(0, QUARTER)
        quantise_h(0, HALF, QUARTER)
        interleave(1, HALF, QUARTER)
        scores(QUARTER, QUARTER)
        quantise_h(1, HALF, QUARTER)
        interleave(0, last_quarter, QUARTER)
        interleave(1, last_quarter, EIGHTH)
        quantise_h(0, last_quarter, QUARTER)
        interleave(1, last_eighth, EIGHTH)
        quantise_h(1, last_quarter, EIGHTH)
        scores(HALF, QUARTER)
        quantise_h(1, last_eighth, EIGHTH)
        scores(last_quarter, EIGHTH)
        scores(last_eighth, EIGHTH)
